import numpy as np
import ml_dtypes


def mxq(x, axis, fmt="e4m3"):
    dtype, down = {"e4m3": (ml_dtypes.float8_e4m3fn, 7), "e5m2": (ml_dtypes.float8_e5m2, 14)}[fmt]
    v = np.moveaxis(np.asarray(x, np.float32).astype(ml_dtypes.bfloat16).astype(np.float64), axis, -1)
    blocks = v.reshape(v.shape[:-1] + (-1, 32))
    amax = np.abs(blocks).max(-1, keepdims=True)
    byte = np.maximum(np.where(amax > 0, np.frexp(amax)[1] - 1 + 127, 0) - down, 1)
    scale = np.exp2(byte - 127.0)
    codes = (blocks / scale).astype(np.float32).astype(dtype).astype(np.float64)
    return np.moveaxis((codes * scale).reshape(v.shape), -1, axis)


WIDE = False


def mx_kscale(k):
    if not WIDE:
        return np.ones(k)
    levels = np.array([10, -10, 5, -5, 0])
    if k % 512:
        return np.exp2(np.random.permutation(np.resize(levels, k // 32))).repeat(32)
    a = np.empty((k // 512, 16))
    for p in range(k // 512):
        a[p, :8] = np.random.permutation(np.resize(levels, 8))
        for g in range(8):
            far = levels[np.abs(levels - a[p, g]) >= 10]
            a[p, g + 8] = far[np.random.randint(len(far))]
    return np.exp2(a.ravel()).repeat(32)


def f64(x):
    return np.asarray(x).astype(np.float64)


def striped(idx):
    return np.tile(idx.reshape(-1, 16).T, (8, 1)).astype(np.uint16)


def unstriped(offs):
    return offs[:16].T.reshape(-1).astype(np.int64)


def striped8(idx):
    return np.concatenate([x.reshape(-1, 16).T for x in idx]).astype(np.uint16)


def runs(offs, k):
    lists = np.stack([offs[16 * r : 16 * r + 16].T.reshape(-1) for r in range(8)]).astype(np.int64)
    return lists[np.arange(k) % 512 // 64]


def pack_weight(w):
    k, n = w.shape
    w = f64(np.asarray(w, np.float32).astype(ml_dtypes.bfloat16)).reshape(k // 32, 32, n)
    amax = np.abs(w).max(1)
    byte = np.clip(np.where(amax > 0, np.frexp(amax)[1] - 1 + 127 - 7, 1), 1, 254)
    scaled = (w * np.exp2(127.0 - byte)[:, None, :]).reshape(k, n).astype(np.float32)
    words = np.ascontiguousarray(scaled.reshape(k // 512, 128, 4, n).transpose(0, 1, 3, 2)).astype(ml_dtypes.float8_e4m3fn).view(np.uint8)
    return words, np.ascontiguousarray(byte.astype(np.uint8).reshape(k // 512, 16, n))


def unpack_weight(words, scales):
    g, p, n, _ = words.shape
    vals = np.ascontiguousarray(words).view(ml_dtypes.float8_e4m3fn).astype(np.float64) * np.repeat(np.exp2(scales.astype(np.float64) - 127.0), 8, axis=1)[..., None]
    return vals.transpose(0, 1, 3, 2).reshape(g * 512, n)

def planes(y):
    n, m = y.shape
    v = y.astype(np.float32).astype(ml_dtypes.bfloat16).astype(np.float64).reshape(n // 32, 32, m)
    top = np.abs(v).max(1)
    byte = np.clip(np.where(top > 0, np.frexp(top)[1] - 1 + 127 - 7, 1), 1, 254)
    codes = (v * np.exp2(127.0 - byte)[:, None, :]).reshape(n, m).astype(np.float32).astype(ml_dtypes.float8_e4m3fn).view(np.uint8)
    words = codes.reshape(n // 512, 128, 4, m).transpose(0, 1, 3, 2)
    return np.ascontiguousarray(words), np.ascontiguousarray(byte.astype(np.uint8).reshape(n // 512, 16, m))


K, T, S, N, H, W = 512, 2048, 256, 512, 512, 1024


def setup_inputs():
    n = np.random.standard_normal
    s = mx_kscale(K)[:, None]
    u = mx_kscale(H)
    packed_xT = pack_weight(n((K, T)) * s)
    packed_w1 = pack_weight(n((K, H)) / np.sqrt(K) / s)
    packed_w2 = pack_weight(n((H, N)) / np.sqrt(2 * H) / u[:, None])
    packed_w3 = pack_weight(n((K, N)) / np.sqrt(2 * K) / s)
    return {
        "x_words": packed_xT[0],
        "x_scales": packed_xT[1],
        "w1_words": packed_w1[0],
        "w1_scales": packed_w1[1],
        "gn": (np.random.uniform(0.5, 1.5, (H, 1)) * u[:, None]).astype(np.float32),
        "w2_words": packed_w2[0],
        "w2_scales": packed_w2[1],
        "w3_words": packed_w3[0],
        "w3_scales": packed_w3[1],
        "offs": striped(np.random.permutation(T)[:S]),
        "n1": striped(np.random.randint(0, S, W)),
        "two": striped(np.random.permutation(T)[:S]),
        "n2": striped8(np.stack([np.random.permutation(S) for _ in range(8)])),
        "n3": striped8(np.stack([np.random.permutation(S) for _ in range(8)])),
    }


def reference(x_words, x_scales, w1_words, w1_scales, gn, w2_words, w2_scales, w3_words, w3_scales, offs, n1, two, n2, n3):
    xq = unpack_weight(x_words, x_scales)[:, unstriped(offs)]
    y = unpack_weight(w1_words, w1_scales).T @ xq
    mb = y[:, unstriped(n1)]
    mn = mb.reshape(H, S, 4).min(axis=2)
    mx = mb.reshape(H, S, 4).max(axis=2)
    z = f64(gn) * (np.maximum(y, mn) - (0.5 * mx))
    x_two = unpack_weight(x_words, x_scales)[:, unstriped(two)]
    h = unpack_weight(w2_words, w2_scales).T @ mxq(z, 0, "e4m3") + unpack_weight(w3_words, w3_scales).T @ x_two
    st = np.maximum(h, h[np.arange(N)[:, None], runs(n2, N)])
    out_0 = np.minimum(st, st[np.arange(N)[:, None], runs(n3, N)])
    return (out_0,) + planes(out_0)

@@ -1,0 +1,246 @@
+from contextlib import ExitStack
+from functools import partial
+
+import concourse.mybir as mybir
+
+K, T, S, N, H, W = 512, 2048, 256, 512, 512, 1024
+FLOPS = 2 * S * (K * H + H * N + K * N)
+
+F32 = mybir.dt.float32
+BF16 = mybir.dt.bfloat16
+I32 = mybir.dt.int32
+U32 = mybir.dt.uint32
+U16 = mybir.dt.uint16
+U8 = mybir.dt.uint8
+FP8X4 = mybir.dt.float8_e4m3fn_x4
+ALU = mybir.AluOpType
+COPY = mybir.ActivationFunctionType.Copy
+
+P = 128
+PACK = 4
+QUAD = 32
+ROWS = 4
+HALF = S // 2
+MEMBERS = 4
+LIST = 16
+Y_WINDOW = MEMBERS * HALF + 32
+H_WINDOW = 2 * S
+
+
+def tile_picked_mixingmidhopmn_none_po_kernel(
+    tc, x_words, x_scales, w1_words, w1_scales, gn, w2_words, w2_scales, w3_words, w3_scales,
+    offs, n1, two, n2, n3, out_0, out_1, out_2,
+):
+    nc = tc.nc
+    with ExitStack() as ctx:
+        lists = ctx.enter_context(tc.tile_pool(name="lists", bufs=1))
+        keep = ctx.enter_context(tc.tile_pool(name="keep", bufs=1))
+        psum = ctx.enter_context(tc.psum_pool(name="psum", bufs=1))
+
+        def sb(name, shape, dtype):
+            return keep.tile(shape, dtype, name=name, align_bytes=64)
+
+        def load_list(name, src):
+            tile = lists.tile(list(src.shape), U16, name=name)
+            nc.sync.dma_start(tile[:], src)
+            return tile
+
+        def load_words(name, src, tag):
+            tile = keep.tile([P, src.shape[2]], I32, name=name, tag=tag, align_bytes=64)
+            nc.sync.dma_start(tile[:], src[0].rearrange("p c r -> p (c r)").bitcast(I32))
+            return tile
+
+        def load_scales(queue, tile, first, src):
+            for q in range(P // QUAD):
+                rows = slice(QUAD * q + first, QUAD * q + first + ROWS)
+                queue.dma_start(tile[rows, :].bitcast(I32), src[0, ROWS * q : ROWS * (q + 1), :].bitcast(I32))
+
+        def deal(name, raw, dtype):
+            dealt = sb(name, [P, PACK, P], dtype)
+            nc.vector.tensor_copy(
+                dealt[:].rearrange("p t m -> p m t"),
+                raw[:].bitcast(dtype).rearrange("p (m t) -> p m t", t=PACK),
+            )
+            return dealt
+
+        xs = sb("xs", [P, T], U8)
+        nc.gpsimd.memset(xs[:].bitcast(I32), 0)
+        w1s = keep.tile([P, H], U8, name="w1s", tag="stage_b", align_bytes=64)
+        for q in range(P // QUAD):
+            queue = nc.gpsimd if q < 2 else nc.scalar
+            queue.dma_start(
+                w1s[QUAD * q : QUAD * (q + 1), :].bitcast(I32),
+                w1_scales[0, ROWS * q : ROWS * (q + 1), :].bitcast(I32).unsqueeze(0).broadcast_to([QUAD // ROWS, ROWS, H // 4]),
+            )
+        offs_t = load_list("offs_t", offs)
+        w1w = load_words("w1w", w1_words, "stage_a")
+        two_t = load_list("two_t", two)
+        xw = load_words("xw", x_words, "xw")
+        load_scales(nc.scalar, xs, 0, x_scales)
+        n1_t = load_list("n1_t", n1)
+        n2_t = load_list("n2_t", n2)
+        n3_t = load_list("n3_t", n3)
+
+        y = [sb("y%d" % t, [P, Y_WINDOW], F32) for t in range(PACK)]
+        h = [sb("h%d" % t, [P, H_WINDOW], F32) for t in range(PACK)]
+        for t in range(PACK):
+            nc.gpsimd.memset(y[t][:, S:], 0.0)
+        w32s = sb("w32s", [P, N], U8)
+        nc.gpsimd.memset(w32s[:].bitcast(I32), 0)
+        gain = sb("gain", [P, PACK], F32)
+        nc.gpsimd.dma_start(gain[:], gn.rearrange("(p t) o -> p (t o)", t=PACK))
+        for t in range(PACK):
+            nc.gpsimd.memset(h[t][:, S:], 0.0)
+
+        def pick(name, offsets):
+            scales = sb(name + "_s", [P, S], U8)
+            words = sb(name + "_w", [P, S], U32)
+            nc.vector.tensor_copy(scales[:], xs[:].indirect(offsets[:]))
+            nc.vector.tensor_copy(words[:], xw[:].bitcast(U32).indirect(offsets[:]))
+            return words, scales
+
+        w1d = deal("w1d", w1w, U32)
+        w1sd = deal("w1sd", w1s, U8)
+        w3w = load_words("w3w", w3_words, "stage_a")
+        w2w = load_words("w2w", w2_words, "stage_b")
+        load_scales(nc.sync, w32s, 0, w3_scales)
+        load_scales(nc.sync, w32s, ROWS, w2_scales)
+        xq_w, xq_s = pick("xq", offs_t)
+        for t in range(PACK):
+            bank = psum.tile([P, S], F32, name="bank%d" % t)
+            nc.tensor.matmul_mx(
+                out=bank[:], lhsT=w1d[:, t, :].bitcast(FP8X4), lhsT_scale=w1sd[:, t, :],
+                rhs=xq_w[:].bitcast(FP8X4), rhs_scale=xq_s[:], start=True, stop=True,
+            )
+            nc.scalar.copy(y[t][:, :S], bank[:])
+
+        x2_w, x2_s = pick("x2", two_t)
+        w3d = deal("w3d", w3w, U32)
+        w2d = deal("w2d", w2w, U32)
+        w32sd = deal("w32sd", w32s, U8)
+
+        def w3_pass(acc, t, cols):
+            nc.tensor.matmul_mx(
+                out=acc, lhsT=w3d[:, t, :].bitcast(FP8X4), lhsT_scale=w32sd[:, t, :],
+                rhs=x2_w[:, cols].bitcast(FP8X4), rhs_scale=x2_s[:, cols], start=True, stop=False,
+            )
+
+        def w2_pass(acc, t, z_w, z_s):
+            nc.tensor.matmul_mx(
+                out=acc, lhsT=w2d[:, t, :].bitcast(FP8X4), lhsT_scale=w32sd[ROWS:, t, :],
+                rhs=z_w[:].bitcast(FP8X4), rhs_scale=z_s[:], start=False, stop=True,
+            )
+
+        def interleaved(grouped):
+            return grouped.rearrange("p (c i) t -> p c t i", i=4)
+
+        def by_fours(planes):
+            return planes.rearrange("p t (c i) -> p c t i", i=4)
+
+        def finish(t, cols, d, mx, top):
+            nc.vector.scalar_tensor_tensor(d[:, t, cols], mx[:], -0.5, top[:], ALU.mult, ALU.add)
+
+        def scale_round(z, d, cols):
+            width = cols.stop - cols.start
+            nc.vector.tensor_tensor(
+                interleaved(z[:, cols, :]), by_fours(d[:, :, cols]),
+                gain[:].unsqueeze(1).unsqueeze(3).broadcast_to([P, width // 4, PACK, 4]), ALU.mult,
+            )
+
+        def quantise(z_w, z_s, z, cols):
+            nc.vector.quantize_mx(
+                out=z_w[:, cols].bitcast(FP8X4), scales=z_s[:, cols], in_=z[:, cols, :].rearrange("p j t -> p (j t)")
+            )
+
+        def make_z(half, pieces):
+            base = HALF * half
+            d = sb("d%d" % half, [P, PACK, HALF], F32)
+            z = sb("z%d" % half, [P, HALF, PACK], BF16)
+            z_w = sb("z_w%d" % half, [P, HALF], U32)
+            z_s = sb("z_s%d" % half, [P, HALF], U8)
+            waiting = []
+            for t, cols in pieces:
+                width = cols.stop - cols.start
+                tag = "%d_%d_%d" % (half, t, cols.start)
+                mb = sb("mb" + tag, [P, width, MEMBERS], F32)
+                entries = slice(MEMBERS * (base + cols.start) // LIST, MEMBERS * (base + cols.stop) // LIST)
+                nc.scalar.activation(mb[:].rearrange("p j e -> p (j e)"), y[t][:].indirect(n1_t[:, entries]), COPY)
+                lo = sb("lo" + tag, [P, width, 2], F32)
+                hi = sb("hi" + tag, [P, width, 2], F32)
+                mn = sb("mn" + tag, [P, width], F32)
+                mx = sb("mx" + tag, [P, width], F32)
+                top = sb("top" + tag, [P, width], F32)
+                steps = [
+                    partial(nc.vector.tensor_tensor, lo[:], mb[:, :, 0:2], mb[:, :, 2:4], ALU.min),
+                    partial(nc.vector.tensor_tensor, hi[:], mb[:, :, 0:2], mb[:, :, 2:4], ALU.max),
+                    partial(nc.vector.tensor_tensor, mn[:], lo[:, :, 0], lo[:, :, 1], ALU.min),
+                    partial(nc.vector.tensor_tensor, mx[:], hi[:, :, 0], hi[:, :, 1], ALU.max),
+                    partial(nc.vector.tensor_tensor, top[:], y[t][:, base + cols.start : base + cols.stop], mn[:], ALU.max),
+                ]
+                for i, step in enumerate(steps):
+                    step()
+                    if i in (1, 3, 4) and waiting:
+                        waiting.pop(0)()
+                waiting.append(partial(finish, t, cols, d, mx, top))
+                if t == PACK - 1:
+                    waiting.append(partial(scale_round, z, d, cols))
+                    waiting.append(partial(quantise, z_w, z_s, z, cols))
+            return z_w, z_s, waiting
+
+        first, second = slice(0, HALF), slice(HALF, S)
+        late = []
+        for t in range(PACK):
+            bank = psum.tile([P, S], F32, name="bank%d" % t)
+            w3_pass(bank[:, :HALF], t, second)
+            late.append(bank)
+
+        whole, left, right = slice(0, HALF), slice(0, HALF // 2), slice(HALF // 2, HALF)
+        z_w, z_s, waiting = make_z(0, [(0, left), (0, right), (1, whole), (2, whole), (3, whole)])
+        for step in waiting:
+            step()
+        early = psum.tile([P, PACK, HALF], F32, name="early")
+        for t in range(PACK):
+            w3_pass(early[:, t, :], t, first)
+            w2_pass(early[:, t, :], t, z_w, z_s)
+        z_w, z_s, waiting = make_z(1, [(0, whole), (1, whole), (2, whole), (3, left), (3, right)])
+        for step in waiting:
+            step()
+        for t in range(PACK):
+            nc.scalar.copy(h[t][:, first], early[:, t, :])
+        for t in range(PACK):
+            w2_pass(late[t][:, :HALF], t, z_w, z_s)
+            nc.vector.tensor_copy(h[t][:, second], late[t][:, :HALF])
+
+        st = []
+        for t in range(PACK):
+            g = sb("g2_%d" % t, [P, S], F32)
+            nc.scalar.activation(g[:], h[t][:].indirect(n2_t[:]), COPY)
+            s = sb("st%d" % t, [P, S], F32)
+            nc.vector.tensor_tensor(s[:], h[t][:, :S], g[:], ALU.max)
+            st.append(s)
+
+        out_rows = out_0.rearrange("(p t) j -> p t j", t=PACK)
+        out_words = out_1[0].rearrange("p c r -> p (c r)").bitcast(I32)
+        o_w = sb("o_w", [P, S], U32)
+        o_s = sb("o_s", [P, S], U8)
+        for half in range(2):
+            cols = slice(HALF * half, HALF * (half + 1))
+            o = sb("o%d" % half, [P, PACK, HALF], F32)
+            per = HALF // LIST
+            for t in range(PACK):
+                g = sb("g3_%d_%d" % (half, t), [P, HALF], F32)
+                nc.scalar.activation(g[:], st[t][:].indirect(n3_t[:, per * half : per * (half + 1)]), COPY)
+                nc.vector.tensor_tensor(o[:, t, :], st[t][:, cols], g[:], ALU.min)
+                if t % 2 == 1:
+                    nc.sync.dma_start(out_rows[:, t - 1 : t + 1, cols], o[:, t - 1 : t + 1, :])
+            ob = sb("ob%d" % half, [P, HALF, PACK], BF16)
+            nc.vector.tensor_copy(interleaved(ob[:]), by_fours(o[:]))
+            nc.vector.quantize_mx(
+                out=o_w[:, cols].bitcast(FP8X4), scales=o_s[:, cols], in_=ob[:].rearrange("p j t -> p (j t)")
+            )
+            nc.sync.dma_start(out_words[:, cols], o_w[:, cols].bitcast(I32))
+        for q in range(P // QUAD):
+            queue = nc.scalar if q % 2 == 0 else nc.sync
+            queue.dma_start(
+                out_2[0, ROWS * q : ROWS * (q + 1), :].bitcast(I32), o_s[QUAD * q : QUAD * q + ROWS, :].bitcast(I32)
+            )

@@ -23,7 +23,7 @@ ROWS = 4
 HALF = S // 2
 MEMBERS = 4
 LIST = 16
-Y_WINDOW = MEMBERS * HALF + 32
+Y_BLOCKS = 5
 H_WINDOW = 2 * S
 
 
@@ -65,56 +65,53 @@ def tile_picked_mixingmidhopmn_none_po_kernel(
 
         xs = sb("xs", [P, T], U8)
         nc.gpsimd.memset(xs[:].bitcast(I32), 0)
-        w1s = keep.tile([P, H], U8, name="w1s", tag="stage_b", align_bytes=64)
+        offs_t = load_list("offs_t", offs)
+        gain = sb("gain", [P, PACK], F32)
+        nc.sync.dma_start(gain[:], gn.rearrange("(p t) o -> p (t o)", t=PACK))
+        w1w = load_words("w1w", w1_words, "w1w")
+        w1s = sb("w1s", [P, H], U8)
         for q in range(P // QUAD):
-            queue = nc.gpsimd if q < 2 else nc.scalar
-            queue.dma_start(
+            nc.sync.dma_start(
                 w1s[QUAD * q : QUAD * (q + 1), :].bitcast(I32),
                 w1_scales[0, ROWS * q : ROWS * (q + 1), :].bitcast(I32).unsqueeze(0).broadcast_to([QUAD // ROWS, ROWS, H // 4]),
             )
-        offs_t = load_list("offs_t", offs)
-        w1w = load_words("w1w", w1_words, "stage_a")
-        two_t = load_list("two_t", two)
         xw = load_words("xw", x_words, "xw")
-        load_scales(nc.scalar, xs, 0, x_scales)
+        load_scales(nc.sync, xs, 0, x_scales)
+        two_t = load_list("two_t", two)
         n1_t = load_list("n1_t", n1)
+        w3w = load_words("w3w", w3_words, "w3w")
+        w2w = load_words("w2w", w2_words, "w2w")
+
+        y = [sb("y%d" % t, [P, Y_BLOCKS, HALF], F32) for t in range(PACK)]
+        h = [sb("h%d" % t, [P, H_WINDOW], F32) for t in range(PACK)]
+        for t in range(PACK):
+            nc.gpsimd.memset(y[t][:, 2:, :], 0.0)
+        w32s = sb("w32s", [P, N], U8)
+        nc.gpsimd.memset(w32s[:].bitcast(I32), 0)
+        load_scales(nc.sync, w32s, 0, w3_scales)
+        load_scales(nc.sync, w32s, ROWS, w2_scales)
         n2_t = load_list("n2_t", n2)
         n3_t = load_list("n3_t", n3)
 
-        y = [sb("y%d" % t, [P, Y_WINDOW], F32) for t in range(PACK)]
-        h = [sb("h%d" % t, [P, H_WINDOW], F32) for t in range(PACK)]
-        for t in range(PACK):
-            nc.gpsimd.memset(y[t][:, S:], 0.0)
-        w32s = sb("w32s", [P, N], U8)
-        nc.gpsimd.memset(w32s[:].bitcast(I32), 0)
-        gain = sb("gain", [P, PACK], F32)
-        nc.gpsimd.dma_start(gain[:], gn.rearrange("(p t) o -> p (t o)", t=PACK))
-        for t in range(PACK):
-            nc.gpsimd.memset(h[t][:, S:], 0.0)
-
-        def pick(name, offsets):
-            scales = sb(name + "_s", [P, S], U8)
-            words = sb(name + "_w", [P, S], U32)
-            nc.vector.tensor_copy(scales[:], xs[:].indirect(offsets[:]))
-            nc.vector.tensor_copy(words[:], xw[:].bitcast(U32).indirect(offsets[:]))
-            return words, scales
+        def pick(name, table, offsets, dtype):
+            picked = sb(name, [P, S], dtype)
+            nc.vector.tensor_copy(picked[:], table[:].bitcast(dtype).indirect(offsets[:]))
+            return picked
 
         w1d = deal("w1d", w1w, U32)
         w1sd = deal("w1sd", w1s, U8)
-        w3w = load_words("w3w", w3_words, "stage_a")
-        w2w = load_words("w2w", w2_words, "stage_b")
-        load_scales(nc.sync, w32s, 0, w3_scales)
-        load_scales(nc.sync, w32s, ROWS, w2_scales)
-        xq_w, xq_s = pick("xq", offs_t)
+        xq_w = pick("xq_w", xw, offs_t, U32)
+        xq_s = pick("xq_s", xs, offs_t, U8)
         for t in range(PACK):
             bank = psum.tile([P, S], F32, name="bank%d" % t)
             nc.tensor.matmul_mx(
                 out=bank[:], lhsT=w1d[:, t, :].bitcast(FP8X4), lhsT_scale=w1sd[:, t, :],
                 rhs=xq_w[:].bitcast(FP8X4), rhs_scale=xq_s[:], start=True, stop=True,
             )
-            nc.scalar.copy(y[t][:, :S], bank[:])
+            nc.scalar.copy(y[t][:, 0:2, :], bank[:].rearrange("p (b j) -> p b j", b=2))
 
-        x2_w, x2_s = pick("x2", two_t)
+        x2_w = pick("x2_w", xw, two_t, U32)
+        x2_s = pick("x2_s", xs, two_t, U8)
         w3d = deal("w3d", w3w, U32)
         w2d = deal("w2d", w2w, U32)
         w32sd = deal("w32sd", w32s, U8)
@@ -137,55 +134,64 @@ def tile_picked_mixingmidhopmn_none_po_kernel(
         def by_fours(planes):
             return planes.rearrange("p t (c i) -> p c t i", i=4)
 
-        def finish(t, cols, d, mx, top):
-            nc.vector.scalar_tensor_tensor(d[:, t, cols], mx[:], -0.5, top[:], ALU.mult, ALU.add)
+        pair = [sb("pair%d" % half, [P, PACK, 2, HALF], F32) for half in range(2)]
+        d = [sb("d%d" % half, [P, PACK, HALF], F32) for half in range(2)]
+        z = [sb("z%d" % half, [P, HALF, PACK], BF16) for half in range(2)]
+        z_w = [sb("z_w%d" % half, [P, HALF], U32) for half in range(2)]
+        z_s = [sb("z_s%d" % half, [P, HALF], U8) for half in range(2)]
 
-        def scale_round(z, d, cols):
+        def members(half, t, cols):
             width = cols.stop - cols.start
+            mb = sb("mb%d_%d_%d" % (half, t, cols.start), [P, width, MEMBERS], F32)
+            entries = slice(MEMBERS * (HALF * half + cols.start) // LIST, MEMBERS * (HALF * half + cols.stop) // LIST)
+            nc.scalar.activation(
+                mb[:].rearrange("p j e -> p (j e)"), y[t][:].rearrange("p b j -> p (b j)").indirect(n1_t[:, entries]), COPY
+            )
+            return mb
+
+        def lows(t, cols):
+            return h[t][:, S:].rearrange("p (j e) -> p j e", e=2)[:, cols, :]
+
+        def pair_min(mb, t, cols):
+            nc.vector.tensor_tensor(lows(t, cols), mb[:, :, 0:2], mb[:, :, 2:4], ALU.min)
+
+        def pair_max(mb, t, cols):
+            nc.vector.tensor_tensor(y[t][:, 3:5, cols].rearrange("p e j -> p j e"), mb[:, :, 0:2], mb[:, :, 2:4], ALU.max)
+
+        def smallest(t, cols):
+            nc.vector.tensor_tensor(y[t][:, 2, cols], lows(t, cols)[:, :, 0], lows(t, cols)[:, :, 1], ALU.min)
+
+        def larger(half, t, cols):
             nc.vector.tensor_tensor(
-                interleaved(z[:, cols, :]), by_fours(d[:, :, cols]),
-                gain[:].unsqueeze(1).unsqueeze(3).broadcast_to([P, width // 4, PACK, 4]), ALU.mult,
+                pair[half][:, t, :, cols], y[t][:, half : Y_BLOCKS : Y_BLOCKS - 1 - half, cols], y[t][:, 2:4, cols], ALU.max
             )
 
-        def quantise(z_w, z_s, z, cols):
+        def difference(half, tiles, cols):
+            nc.vector.scalar_tensor_tensor(
+                d[half][:, tiles, cols], pair[half][:, tiles, 1, cols], -0.5, pair[half][:, tiles, 0, cols], ALU.mult, ALU.add
+            )
+
+        def scale_round(half, cols):
+            nc.vector.tensor_tensor(
+                interleaved(z[half][:, cols, :]), by_fours(d[half][:, :, cols]),
+                gain[:].unsqueeze(1).unsqueeze(3).broadcast_to([P, (cols.stop - cols.start) // 4, PACK, 4]), ALU.mult,
+            )
+
+        def quantise(half, cols):
             nc.vector.quantize_mx(
-                out=z_w[:, cols].bitcast(FP8X4), scales=z_s[:, cols], in_=z[:, cols, :].rearrange("p j t -> p (j t)")
+                out=z_w[half][:, cols].bitcast(FP8X4), scales=z_s[half][:, cols],
+                in_=z[half][:, cols, :].rearrange("p j t -> p (j t)"),
             )
 
-        def make_z(half, pieces):
-            base = HALF * half
-            d = sb("d%d" % half, [P, PACK, HALF], F32)
-            z = sb("z%d" % half, [P, HALF, PACK], BF16)
-            z_w = sb("z_w%d" % half, [P, HALF], U32)
-            z_s = sb("z_s%d" % half, [P, HALF], U8)
-            waiting = []
-            for t, cols in pieces:
-                width = cols.stop - cols.start
-                tag = "%d_%d_%d" % (half, t, cols.start)
-                mb = sb("mb" + tag, [P, width, MEMBERS], F32)
-                entries = slice(MEMBERS * (base + cols.start) // LIST, MEMBERS * (base + cols.stop) // LIST)
-                nc.scalar.activation(mb[:].rearrange("p j e -> p (j e)"), y[t][:].indirect(n1_t[:, entries]), COPY)
-                lo = sb("lo" + tag, [P, width, 2], F32)
-                hi = sb("hi" + tag, [P, width, 2], F32)
-                mn = sb("mn" + tag, [P, width], F32)
-                mx = sb("mx" + tag, [P, width], F32)
-                top = sb("top" + tag, [P, width], F32)
-                steps = [
-                    partial(nc.vector.tensor_tensor, lo[:], mb[:, :, 0:2], mb[:, :, 2:4], ALU.min),
-                    partial(nc.vector.tensor_tensor, hi[:], mb[:, :, 0:2], mb[:, :, 2:4], ALU.max),
-                    partial(nc.vector.tensor_tensor, mn[:], lo[:, :, 0], lo[:, :, 1], ALU.min),
-                    partial(nc.vector.tensor_tensor, mx[:], hi[:, :, 0], hi[:, :, 1], ALU.max),
-                    partial(nc.vector.tensor_tensor, top[:], y[t][:, base + cols.start : base + cols.stop], mn[:], ALU.max),
-                ]
-                for i, step in enumerate(steps):
-                    step()
-                    if i in (1, 3, 4) and waiting:
-                        waiting.pop(0)()
-                waiting.append(partial(finish, t, cols, d, mx, top))
-                if t == PACK - 1:
-                    waiting.append(partial(scale_round, z, d, cols))
-                    waiting.append(partial(quantise, z_w, z_s, z, cols))
-            return z_w, z_s, waiting
+        def piece(half, t, cols, after_min, after_smallest):
+            mb = members(half, t, cols)
+            pair_min(mb, t, cols)
+            for step in after_min:
+                step()
+            pair_max(mb, t, cols)
+            smallest(t, cols)
+            for step in after_smallest:
+                step()
 
         first, second = slice(0, HALF), slice(HALF, S)
         late = []
@@ -193,23 +199,44 @@ def tile_picked_mixingmidhopmn_none_po_kernel(
             bank = psum.tile([P, S], F32, name="bank%d" % t)
             w3_pass(bank[:, :HALF], t, second)
             late.append(bank)
+        early = psum.tile([P, PACK, HALF], F32, name="early")
+
+        def first_products():
+            quantise(0, whole)
+            for t in range(PACK):
+                w3_pass(early[:, t, :], t, first)
+                w2_pass(early[:, t, :], t, z_w[0], z_s[0])
+
+        def second_products():
+            for t in range(PACK):
+                nc.scalar.copy(h[t][:, first], early[:, t, :])
+            for t in range(PACK):
+                w2_pass(late[t][:, :HALF], t, z_w[1], z_s[1])
+                nc.vector.tensor_copy(h[t][:, second], late[t][:, :HALF])
 
         whole, left, right = slice(0, HALF), slice(0, HALF // 2), slice(HALF // 2, HALF)
-        z_w, z_s, waiting = make_z(0, [(0, left), (0, right), (1, whole), (2, whole), (3, whole)])
-        for step in waiting:
-            step()
-        early = psum.tile([P, PACK, HALF], F32, name="early")
-        for t in range(PACK):
-            w3_pass(early[:, t, :], t, first)
-            w2_pass(early[:, t, :], t, z_w, z_s)
-        z_w, z_s, waiting = make_z(1, [(0, whole), (1, whole), (2, whole), (3, left), (3, right)])
-        for step in waiting:
-            step()
-        for t in range(PACK):
-            nc.scalar.copy(h[t][:, first], early[:, t, :])
-        for t in range(PACK):
-            w2_pass(late[t][:, :HALF], t, z_w, z_s)
-            nc.vector.tensor_copy(h[t][:, second], late[t][:, :HALF])
+        piece(0, 0, whole, [], [])
+        for t in range(1, PACK):
+            piece(0, t, whole, [partial(larger, 0, t - 1, whole)], [])
+        piece(1, 0, whole, [partial(larger, 0, 3, whole)], [partial(difference, 0, slice(0, PACK), whole)])
+        piece(1, 1, whole, [partial(larger, 1, 0, whole)], [partial(scale_round, 0, whole)])
+        piece(1, 2, whole, [partial(larger, 1, 1, whole)], [first_products])
+        mb = members(1, 3, left)
+        apart = sb("apart", [P, 3, HALF // 2], F32)
+        pair_min(mb, 3, left)
+        larger(1, 2, whole)
+        nc.vector.tensor_tensor(apart[:, 1:3, :].rearrange("p e j -> p j e"), mb[:, :, 0:2], mb[:, :, 2:4], ALU.max)
+        nc.vector.tensor_tensor(apart[:, 0, :], lows(3, left)[:, :, 0], lows(3, left)[:, :, 1], ALU.min)
+        difference(1, slice(0, 3), whole)
+        nc.vector.tensor_tensor(pair[1][:, 3, 0, left], y[3][:, 1, left], apart[:, 0, :], ALU.max)
+        nc.vector.tensor_tensor(pair[1][:, 3, 1, left], apart[:, 1, :], apart[:, 2, :], ALU.max)
+        piece(1, 3, right, [partial(difference, 1, slice(3, 4), left)], [partial(scale_round, 1, left)])
+        larger(1, 3, right)
+        quantise(1, left)
+        difference(1, slice(3, 4), right)
+        scale_round(1, right)
+        quantise(1, right)
+        second_products()
 
         st = []
         for t in range(PACK):

@@ -108,25 +108,14 @@ def tile_picked_mixingmidhopmn_none_po_kernel(
                 out=bank[:], lhsT=w1d[:, t, :].bitcast(FP8X4), lhsT_scale=w1sd[:, t, :],
                 rhs=xq_w[:].bitcast(FP8X4), rhs_scale=xq_s[:], start=True, stop=True,
             )
-            nc.scalar.copy(y[t][:, 0:2, :], bank[:].rearrange("p (b j) -> p b j", b=2))
+            empty = nc.scalar.copy if t < 2 else nc.vector.tensor_copy
+            empty(y[t][:, 0:2, :], bank[:].rearrange("p (b j) -> p b j", b=2))
 
         x2_w = pick("x2_w", xw, two_t, U32)
         x2_s = pick("x2_s", xs, two_t, U8)
         w3d = deal("w3d", w3w, U32)
         w2d = deal("w2d", w2w, U32)
         w32sd = deal("w32sd", w32s, U8)
-
-        def w3_pass(acc, t, cols):
-            nc.tensor.matmul_mx(
-                out=acc, lhsT=w3d[:, t, :].bitcast(FP8X4), lhsT_scale=w32sd[:, t, :],
-                rhs=x2_w[:, cols].bitcast(FP8X4), rhs_scale=x2_s[:, cols], start=True, stop=False,
-            )
-
-        def w2_pass(acc, t, z_w, z_s):
-            nc.tensor.matmul_mx(
-                out=acc, lhsT=w2d[:, t, :].bitcast(FP8X4), lhsT_scale=w32sd[ROWS:, t, :],
-                rhs=z_w[:].bitcast(FP8X4), rhs_scale=z_s[:], start=False, stop=True,
-            )
 
         def interleaved(grouped):
             return grouped.rearrange("p (c i) t -> p c t i", i=4)
@@ -137,7 +126,7 @@ def tile_picked_mixingmidhopmn_none_po_kernel(
         pair = [sb("pair%d" % half, [P, PACK, 2, HALF], F32) for half in range(2)]
         d = [sb("d%d" % half, [P, PACK, HALF], F32) for half in range(2)]
         z = [sb("z%d" % half, [P, HALF, PACK], BF16) for half in range(2)]
-        z_w = [sb("z_w%d" % half, [P, HALF], U32) for half in range(2)]
+        z_w = [None, sb("z_w1", [P, HALF], U32)]
         z_s = [sb("z_s%d" % half, [P, HALF], U8) for half in range(2)]
 
         def members(half, t, cols):
@@ -193,34 +182,35 @@ def tile_picked_mixingmidhopmn_none_po_kernel(
             for step in after_smallest:
                 step()
 
-        first, second = slice(0, HALF), slice(HALF, S)
-        late = []
+        acc = []
         for t in range(PACK):
             bank = psum.tile([P, S], F32, name="bank%d" % t)
-            w3_pass(bank[:, :HALF], t, second)
-            late.append(bank)
-        early = psum.tile([P, PACK, HALF], F32, name="early")
+            nc.tensor.matmul_mx(
+                out=bank[:], lhsT=w3d[:, t, :].bitcast(FP8X4), lhsT_scale=w32sd[:, t, :],
+                rhs=x2_w[:].bitcast(FP8X4), rhs_scale=x2_s[:], start=True, stop=False,
+            )
+            acc.append(bank)
 
-        def first_products():
-            quantise(0, whole)
-            for t in range(PACK):
-                w3_pass(early[:, t, :], t, first)
-                w2_pass(early[:, t, :], t, z_w[0], z_s[0])
+        def w2_pass(half, t):
+            nc.tensor.matmul_mx(
+                out=acc[t][:, HALF * half : HALF * (half + 1)], lhsT=w2d[:, t, :].bitcast(FP8X4),
+                lhsT_scale=w32sd[ROWS:, t, :], rhs=z_w[half][:].bitcast(FP8X4), rhs_scale=z_s[half][:],
+                start=False, stop=(half == 1),
+            )
 
-        def second_products():
+        def scale_round_on_scalar(half, cols):
+            planes = sb("planes%d" % half, [P, PACK, cols.stop - cols.start], BF16)
             for t in range(PACK):
-                nc.scalar.copy(h[t][:, first], early[:, t, :])
-            for t in range(PACK):
-                w2_pass(late[t][:, :HALF], t, z_w[1], z_s[1])
-                nc.vector.tensor_copy(h[t][:, second], late[t][:, :HALF])
+                nc.scalar.activation(planes[:, t, :], d[half][:, t, cols], COPY, scale=gain[:, t : t + 1])
+            nc.scalar.copy(interleaved(z[half][:, cols, :]), by_fours(planes[:]))
 
         whole, left, right = slice(0, HALF), slice(0, HALF // 2), slice(HALF // 2, HALF)
         piece(0, 0, whole, [], [])
         for t in range(1, PACK):
             piece(0, t, whole, [partial(larger, 0, t - 1, whole)], [])
         piece(1, 0, whole, [partial(larger, 0, 3, whole)], [partial(difference, 0, slice(0, PACK), whole)])
-        piece(1, 1, whole, [partial(larger, 1, 0, whole)], [partial(scale_round, 0, whole)])
-        piece(1, 2, whole, [partial(larger, 1, 1, whole)], [first_products])
+        piece(1, 1, whole, [partial(larger, 1, 0, whole)], [])
+        piece(1, 2, whole, [partial(larger, 1, 1, whole)], [])
         mb = members(1, 3, left)
         apart = sb("apart", [P, 3, HALF // 2], F32)
         pair_min(mb, 3, left)
@@ -231,12 +221,19 @@ def tile_picked_mixingmidhopmn_none_po_kernel(
         nc.vector.tensor_tensor(pair[1][:, 3, 0, left], y[3][:, 1, left], apart[:, 0, :], ALU.max)
         nc.vector.tensor_tensor(pair[1][:, 3, 1, left], apart[:, 1, :], apart[:, 2, :], ALU.max)
         piece(1, 3, right, [partial(difference, 1, slice(3, 4), left)], [partial(scale_round, 1, left)])
+        scale_round_on_scalar(0, whole)
         larger(1, 3, right)
-        quantise(1, left)
+        z_w[0] = keep.tile([P, HALF], U32, name="z_w0", tag="mb1_3_64", align_bytes=64)
+        quantise(0, whole)
+        for t in range(PACK):
+            w2_pass(0, t)
         difference(1, slice(3, 4), right)
+        quantise(1, left)
         scale_round(1, right)
         quantise(1, right)
-        second_products()
+        for t in range(PACK):
+            w2_pass(1, t)
+            nc.vector.tensor_copy(h[t][:, :S], acc[t][:])
 
         st = []
         for t in range(PACK):
@@ -250,22 +247,49 @@ def tile_picked_mixingmidhopmn_none_po_kernel(
         out_words = out_1[0].rearrange("p c r -> p (c r)").bitcast(I32)
         o_w = sb("o_w", [P, S], U32)
         o_s = sb("o_s", [P, S], U8)
-        for half in range(2):
-            cols = slice(HALF * half, HALF * (half + 1))
-            o = sb("o%d" % half, [P, PACK, HALF], F32)
-            per = HALF // LIST
-            for t in range(PACK):
-                g = sb("g3_%d_%d" % (half, t), [P, HALF], F32)
-                nc.scalar.activation(g[:], st[t][:].indirect(n3_t[:, per * half : per * (half + 1)]), COPY)
-                nc.vector.tensor_tensor(o[:, t, :], st[t][:, cols], g[:], ALU.min)
-                if t % 2 == 1:
-                    nc.sync.dma_start(out_rows[:, t - 1 : t + 1, cols], o[:, t - 1 : t + 1, :])
-            ob = sb("ob%d" % half, [P, HALF, PACK], BF16)
-            nc.vector.tensor_copy(interleaved(ob[:]), by_fours(o[:]))
+        o = [sb("o%d" % half, [P, PACK, HALF], F32) for half in range(2)]
+        ob = [sb("ob%d" % half, [P, HALF, PACK], BF16) for half in range(2)]
+
+        def hop(half, t, cols):
+            place = slice(HALF * half + cols.start, HALF * half + cols.stop)
+            g = sb("g3_%d_%d" % (t, place.start), [P, cols.stop - cols.start], F32)
+            nc.scalar.activation(g[:], st[t][:].indirect(n3_t[:, place.start // LIST : place.stop // LIST]), COPY)
+            nc.vector.tensor_tensor(o[half][:, t, cols], st[t][:, place], g[:], ALU.min)
+
+        def store_values(half, tiles):
+            nc.sync.dma_start(out_rows[:, tiles, HALF * half : HALF * (half + 1)], o[half][:, tiles, :])
+
+        def round_out(half, cols):
+            nc.vector.tensor_copy(interleaved(ob[half][:, cols, :]), by_fours(o[half][:, :, cols]))
+
+        def quantise_out(half, cols):
+            place = slice(HALF * half + cols.start, HALF * half + cols.stop)
             nc.vector.quantize_mx(
-                out=o_w[:, cols].bitcast(FP8X4), scales=o_s[:, cols], in_=ob[:].rearrange("p j t -> p (j t)")
+                out=o_w[:, place].bitcast(FP8X4), scales=o_s[:, place],
+                in_=ob[half][:, cols, :].rearrange("p j t -> p (j t)"),
             )
-            nc.sync.dma_start(out_words[:, cols], o_w[:, cols].bitcast(I32))
+
+        def store_words(half):
+            place = slice(HALF * half, HALF * (half + 1))
+            nc.sync.dma_start(out_words[:, place], o_w[:, place].bitcast(I32))
+
+        for t in range(PACK):
+            hop(0, t, whole)
+        store_values(0, slice(0, PACK))
+        round_out(0, whole)
+        hop(1, 0, whole)
+        quantise_out(0, whole)
+        store_words(0)
+        hop(1, 1, whole)
+        store_values(1, slice(0, 2))
+        hop(1, 2, whole)
+        hop(1, 3, left)
+        hop(1, 3, right)
+        store_values(1, slice(2, 4))
+        round_out(1, left)
+        round_out(1, right)
+        quantise_out(1, whole)
+        store_words(1)
         for q in range(P // QUAD):
             queue = nc.scalar if q % 2 == 0 else nc.sync
             queue.dma_start(

from contextlib import ExitStack
from functools import partial

import concourse.mybir as mybir

K, T, S, N, H, W = 512, 2048, 256, 512, 512, 1024
FLOPS = 2 * S * (K * H + H * N + K * N)

F32 = mybir.dt.float32
BF16 = mybir.dt.bfloat16
I32 = mybir.dt.int32
U32 = mybir.dt.uint32
U16 = mybir.dt.uint16
U8 = mybir.dt.uint8
FP8X4 = mybir.dt.float8_e4m3fn_x4
ALU = mybir.AluOpType
COPY = mybir.ActivationFunctionType.Copy

P = 128
PACK = 4
QUAD = 32
ROWS = 4
HALF = S // 2
MEMBERS = 4
LIST = 16
Y_BLOCKS = 5
H_WINDOW = 2 * S


def tile_picked_mixingmidhopmn_none_po_kernel(
    tc, x_words, x_scales, w1_words, w1_scales, gn, w2_words, w2_scales, w3_words, w3_scales,
    offs, n1, two, n2, n3, out_0, out_1, out_2,
):
    nc = tc.nc
    with ExitStack() as ctx:
        lists = ctx.enter_context(tc.tile_pool(name="lists", bufs=1))
        keep = ctx.enter_context(tc.tile_pool(name="keep", bufs=1))
        psum = ctx.enter_context(tc.psum_pool(name="psum", bufs=1))

        def sb(name, shape, dtype):
            return keep.tile(shape, dtype, name=name, align_bytes=64)

        def load_list(name, src):
            tile = lists.tile(list(src.shape), U16, name=name)
            nc.sync.dma_start(tile[:], src)
            return tile

        def load_words(name, src, tag):
            tile = keep.tile([P, src.shape[2]], I32, name=name, tag=tag, align_bytes=64)
            nc.sync.dma_start(tile[:], src[0].rearrange("p c r -> p (c r)").bitcast(I32))
            return tile

        def load_scales(queue, tile, first, src):
            for q in range(P // QUAD):
                rows = slice(QUAD * q + first, QUAD * q + first + ROWS)
                queue.dma_start(tile[rows, :].bitcast(I32), src[0, ROWS * q : ROWS * (q + 1), :].bitcast(I32))

        def deal(name, raw, dtype):
            dealt = sb(name, [P, PACK, P], dtype)
            nc.vector.tensor_copy(
                dealt[:].rearrange("p t m -> p m t"),
                raw[:].bitcast(dtype).rearrange("p (m t) -> p m t", t=PACK),
            )
            return dealt

        xs = sb("xs", [P, T], U8)
        nc.gpsimd.memset(xs[:].bitcast(I32), 0)
        offs_t = load_list("offs_t", offs)
        gain = sb("gain", [P, PACK], F32)
        nc.sync.dma_start(gain[:], gn.rearrange("(p t) o -> p (t o)", t=PACK))
        w1w = load_words("w1w", w1_words, "w1w")
        w1s = sb("w1s", [P, H], U8)
        for q in range(P // QUAD):
            nc.sync.dma_start(
                w1s[QUAD * q : QUAD * (q + 1), :].bitcast(I32),
                w1_scales[0, ROWS * q : ROWS * (q + 1), :].bitcast(I32).unsqueeze(0).broadcast_to([QUAD // ROWS, ROWS, H // 4]),
            )
        xw = load_words("xw", x_words, "xw")
        load_scales(nc.sync, xs, 0, x_scales)
        two_t = load_list("two_t", two)
        n1_t = load_list("n1_t", n1)
        w3w = load_words("w3w", w3_words, "w3w")
        w2w = load_words("w2w", w2_words, "w2w")

        y = [sb("y%d" % t, [P, Y_BLOCKS, HALF], F32) for t in range(PACK)]
        h = [sb("h%d" % t, [P, H_WINDOW], F32) for t in range(PACK)]
        for t in range(PACK):
            nc.gpsimd.memset(y[t][:, 2:, :], 0.0)
        w32s = sb("w32s", [P, N], U8)
        nc.gpsimd.memset(w32s[:].bitcast(I32), 0)
        load_scales(nc.sync, w32s, 0, w3_scales)
        load_scales(nc.sync, w32s, ROWS, w2_scales)
        n2_t = load_list("n2_t", n2)
        n3_t = load_list("n3_t", n3)

        def pick(name, table, offsets, dtype):
            picked = sb(name, [P, S], dtype)
            nc.vector.tensor_copy(picked[:], table[:].bitcast(dtype).indirect(offsets[:]))
            return picked

        w1d = deal("w1d", w1w, U32)
        w1sd = deal("w1sd", w1s, U8)
        xq_w = pick("xq_w", xw, offs_t, U32)
        xq_s = pick("xq_s", xs, offs_t, U8)
        for t in range(PACK):
            bank = psum.tile([P, S], F32, name="bank%d" % t)
            nc.tensor.matmul_mx(
                out=bank[:], lhsT=w1d[:, t, :].bitcast(FP8X4), lhsT_scale=w1sd[:, t, :],
                rhs=xq_w[:].bitcast(FP8X4), rhs_scale=xq_s[:], start=True, stop=True,
            )
            empty = nc.scalar.copy if t < 2 else nc.vector.tensor_copy
            empty(y[t][:, 0:2, :], bank[:].rearrange("p (b j) -> p b j", b=2))

        x2_w = pick("x2_w", xw, two_t, U32)
        x2_s = pick("x2_s", xs, two_t, U8)
        w3d = deal("w3d", w3w, U32)
        w2d = deal("w2d", w2w, U32)
        w32sd = deal("w32sd", w32s, U8)

        def interleaved(grouped):
            return grouped.rearrange("p (c i) t -> p c t i", i=4)

        def by_fours(planes):
            return planes.rearrange("p t (c i) -> p c t i", i=4)

        pair = [sb("pair%d" % half, [P, PACK, 2, HALF], F32) for half in range(2)]
        d = [sb("d%d" % half, [P, PACK, HALF], F32) for half in range(2)]
        z = [sb("z%d" % half, [P, HALF, PACK], BF16) for half in range(2)]
        z_w = [None, sb("z_w1", [P, HALF], U32)]
        z_s = [sb("z_s%d" % half, [P, HALF], U8) for half in range(2)]

        def members(half, t, cols):
            width = cols.stop - cols.start
            mb = sb("mb%d_%d_%d" % (half, t, cols.start), [P, width, MEMBERS], F32)
            entries = slice(MEMBERS * (HALF * half + cols.start) // LIST, MEMBERS * (HALF * half + cols.stop) // LIST)
            nc.scalar.activation(
                mb[:].rearrange("p j e -> p (j e)"), y[t][:].rearrange("p b j -> p (b j)").indirect(n1_t[:, entries]), COPY
            )
            return mb

        def lows(t, cols):
            return h[t][:, S:].rearrange("p (j e) -> p j e", e=2)[:, cols, :]

        def pair_min(mb, t, cols):
            nc.vector.tensor_tensor(lows(t, cols), mb[:, :, 0:2], mb[:, :, 2:4], ALU.min)

        def pair_max(mb, t, cols):
            nc.vector.tensor_tensor(y[t][:, 3:5, cols].rearrange("p e j -> p j e"), mb[:, :, 0:2], mb[:, :, 2:4], ALU.max)

        def smallest(t, cols):
            nc.vector.tensor_tensor(y[t][:, 2, cols], lows(t, cols)[:, :, 0], lows(t, cols)[:, :, 1], ALU.min)

        def larger(half, t, cols):
            nc.vector.tensor_tensor(
                pair[half][:, t, :, cols], y[t][:, half : Y_BLOCKS : Y_BLOCKS - 1 - half, cols], y[t][:, 2:4, cols], ALU.max
            )

        def difference(half, tiles, cols):
            nc.vector.scalar_tensor_tensor(
                d[half][:, tiles, cols], pair[half][:, tiles, 1, cols], -0.5, pair[half][:, tiles, 0, cols], ALU.mult, ALU.add
            )

        def scale_round(half, cols):
            nc.vector.tensor_tensor(
                interleaved(z[half][:, cols, :]), by_fours(d[half][:, :, cols]),
                gain[:].unsqueeze(1).unsqueeze(3).broadcast_to([P, (cols.stop - cols.start) // 4, PACK, 4]), ALU.mult,
            )

        def quantise(half, cols):
            nc.vector.quantize_mx(
                out=z_w[half][:, cols].bitcast(FP8X4), scales=z_s[half][:, cols],
                in_=z[half][:, cols, :].rearrange("p j t -> p (j t)"),
            )

        def piece(half, t, cols, after_min, after_smallest):
            mb = members(half, t, cols)
            pair_min(mb, t, cols)
            for step in after_min:
                step()
            pair_max(mb, t, cols)
            smallest(t, cols)
            for step in after_smallest:
                step()

        acc = []
        for t in range(PACK):
            bank = psum.tile([P, S], F32, name="bank%d" % t)
            nc.tensor.matmul_mx(
                out=bank[:], lhsT=w3d[:, t, :].bitcast(FP8X4), lhsT_scale=w32sd[:, t, :],
                rhs=x2_w[:].bitcast(FP8X4), rhs_scale=x2_s[:], start=True, stop=False,
            )
            acc.append(bank)

        def w2_pass(half, t):
            nc.tensor.matmul_mx(
                out=acc[t][:, HALF * half : HALF * (half + 1)], lhsT=w2d[:, t, :].bitcast(FP8X4),
                lhsT_scale=w32sd[ROWS:, t, :], rhs=z_w[half][:].bitcast(FP8X4), rhs_scale=z_s[half][:],
                start=False, stop=(half == 1),
            )

        def scale_round_on_scalar(half, cols):
            planes = sb("planes%d" % half, [P, PACK, cols.stop - cols.start], BF16)
            for t in range(PACK):
                nc.scalar.activation(planes[:, t, :], d[half][:, t, cols], COPY, scale=gain[:, t : t + 1])
            nc.scalar.copy(interleaved(z[half][:, cols, :]), by_fours(planes[:]))

        whole, left, right = slice(0, HALF), slice(0, HALF // 2), slice(HALF // 2, HALF)
        piece(0, 0, whole, [], [])
        for t in range(1, PACK):
            piece(0, t, whole, [partial(larger, 0, t - 1, whole)], [])
        piece(1, 0, whole, [partial(larger, 0, 3, whole)], [partial(difference, 0, slice(0, PACK), whole)])
        piece(1, 1, whole, [partial(larger, 1, 0, whole)], [])
        piece(1, 2, whole, [partial(larger, 1, 1, whole)], [])
        mb = members(1, 3, left)
        apart = sb("apart", [P, 3, HALF // 2], F32)
        pair_min(mb, 3, left)
        larger(1, 2, whole)
        nc.vector.tensor_tensor(apart[:, 1:3, :].rearrange("p e j -> p j e"), mb[:, :, 0:2], mb[:, :, 2:4], ALU.max)
        nc.vector.tensor_tensor(apart[:, 0, :], lows(3, left)[:, :, 0], lows(3, left)[:, :, 1], ALU.min)
        difference(1, slice(0, 3), whole)
        nc.vector.tensor_tensor(pair[1][:, 3, 0, left], y[3][:, 1, left], apart[:, 0, :], ALU.max)
        nc.vector.tensor_tensor(pair[1][:, 3, 1, left], apart[:, 1, :], apart[:, 2, :], ALU.max)
        piece(1, 3, right, [partial(difference, 1, slice(3, 4), left)], [partial(scale_round, 1, left)])
        scale_round_on_scalar(0, whole)
        larger(1, 3, right)
        z_w[0] = keep.tile([P, HALF], U32, name="z_w0", tag="mb1_3_64", align_bytes=64)
        quantise(0, whole)
        for t in range(PACK):
            w2_pass(0, t)
        difference(1, slice(3, 4), right)
        quantise(1, left)
        scale_round(1, right)
        quantise(1, right)
        for t in range(PACK):
            w2_pass(1, t)
            nc.vector.tensor_copy(h[t][:, :S], acc[t][:])

        st = []
        for t in range(PACK):
            g = sb("g2_%d" % t, [P, S], F32)
            nc.scalar.activation(g[:], h[t][:].indirect(n2_t[:]), COPY)
            s = sb("st%d" % t, [P, S], F32)
            nc.vector.tensor_tensor(s[:], h[t][:, :S], g[:], ALU.max)
            st.append(s)

        out_rows = out_0.rearrange("(p t) j -> p t j", t=PACK)
        out_words = out_1[0].rearrange("p c r -> p (c r)").bitcast(I32)
        o_w = sb("o_w", [P, S], U32)
        o_s = sb("o_s", [P, S], U8)
        o = [sb("o%d" % half, [P, PACK, HALF], F32) for half in range(2)]
        ob = [sb("ob%d" % half, [P, HALF, PACK], BF16) for half in range(2)]

        def hop(half, t, cols):
            place = slice(HALF * half + cols.start, HALF * half + cols.stop)
            g = sb("g3_%d_%d" % (t, place.start), [P, cols.stop - cols.start], F32)
            nc.scalar.activation(g[:], st[t][:].indirect(n3_t[:, place.start // LIST : place.stop // LIST]), COPY)
            nc.vector.tensor_tensor(o[half][:, t, cols], st[t][:, place], g[:], ALU.min)

        def store_values(half, tiles):
            nc.sync.dma_start(out_rows[:, tiles, HALF * half : HALF * (half + 1)], o[half][:, tiles, :])

        def round_out(half, cols):
            nc.vector.tensor_copy(interleaved(ob[half][:, cols, :]), by_fours(o[half][:, :, cols]))

        def quantise_out(half, cols):
            place = slice(HALF * half + cols.start, HALF * half + cols.stop)
            nc.vector.quantize_mx(
                out=o_w[:, place].bitcast(FP8X4), scales=o_s[:, place],
                in_=ob[half][:, cols, :].rearrange("p j t -> p (j t)"),
            )

        def store_words(half):
            place = slice(HALF * half, HALF * (half + 1))
            nc.sync.dma_start(out_words[:, place], o_w[:, place].bitcast(I32))

        for t in range(PACK):
            hop(0, t, whole)
        store_values(0, slice(0, PACK))
        round_out(0, whole)
        hop(1, 0, whole)
        quantise_out(0, whole)
        store_words(0)
        hop(1, 1, whole)
        store_values(1, slice(0, 2))
        hop(1, 2, whole)
        hop(1, 3, left)
        hop(1, 3, right)
        store_values(1, slice(2, 4))
        round_out(1, left)
        round_out(1, right)
        quantise_out(1, whole)
        store_words(1)
        for q in range(P // QUAD):
            queue = nc.scalar if q % 2 == 0 else nc.sync
            queue.dma_start(
                out_2[0, ROWS * q : ROWS * (q + 1), :].bitcast(I32), o_s[QUAD * q : QUAD * q + ROWS, :].bitcast(I32)
            )
